import numpy as np
import ml_dtypes


def mxq(x, axis, fmt="e4m3"):
    dtype, down = {"e4m3": (ml_dtypes.float8_e4m3fn, 7), "e5m2": (ml_dtypes.float8_e5m2, 14)}[fmt]
    v = np.moveaxis(np.asarray(x, np.float32).astype(ml_dtypes.bfloat16).astype(np.float64), axis, -1)
    blocks = v.reshape(v.shape[:-1] + (-1, 32))
    amax = np.abs(blocks).max(-1, keepdims=True)
    byte = np.maximum(np.where(amax > 0, np.frexp(amax)[1] - 1 + 127, 0) - down, 1)
    scale = np.exp2(byte - 127.0)
    codes = (blocks / scale).astype(np.float32).astype(dtype).astype(np.float64)
    return np.moveaxis((codes * scale).reshape(v.shape), -1, axis)


WIDE = False


def mx_kscale(k):
    if not WIDE:
        return np.ones(k)
    levels = np.array([30, -30])
    if k % 512:
        return np.exp2(np.random.permutation(np.resize(levels, k // 32))).repeat(32)
    a = np.empty((k // 512, 16))
    for p in range(k // 512):
        a[p, :8] = np.random.permutation(np.resize(levels, 8))
        for g in range(8):
            far = levels[np.abs(levels - a[p, g]) >= 10]
            a[p, g + 8] = far[np.random.randint(len(far))]
    return np.exp2(a.ravel()).repeat(32)


def f64(x):
    return np.asarray(x).astype(np.float64)


def striped(idx):
    return np.tile(np.asarray(idx).reshape(-1, 16).T, (8, 1)).astype(np.uint16)


def unstriped(offs):
    return offs[:16].T.reshape(-1).astype(np.int64)


E2M1 = np.array([0.0, 0.5, 1.0, 1.5, 2.0, 3.0, 4.0, 6.0, -0.0, -0.5, -1.0, -1.5, -2.0, -3.0, -4.0, -6.0])


def pack_weight(w, fmt):
    k, n = w.shape
    w = f64(np.asarray(w, np.float32).astype(ml_dtypes.bfloat16)).reshape(k // 32, 32, n)
    amax = np.abs(w).max(1)
    if fmt == "e4m3":
        byte = np.frexp(amax)[1] - 1 + 127 - 7
    else:
        mant, ex = np.frexp(amax / 6.0)
        byte = np.where(mant > 0.5, ex, ex - 1) + 127
    byte = np.clip(np.where(amax > 0, byte, 1), 1, 254)
    scaled = (w * np.exp2(127.0 - byte)[:, None, :]).reshape(k, n).astype(np.float32)
    by_word = np.ascontiguousarray(scaled.reshape(k // 512, 128, 4, n).transpose(0, 1, 3, 2))
    if fmt == "e4m3":
        words = by_word.astype(ml_dtypes.float8_e4m3fn).view(np.uint8)
    else:
        c = by_word.astype(ml_dtypes.float4_e2m1fn).view(np.uint8) & 0xF
        words = (c[..., 0::2] | (c[..., 1::2] << 4)).reshape(k // 512, 128, 2 * n)
    return np.ascontiguousarray(words), np.ascontiguousarray(byte.astype(np.uint8).reshape(k // 512, 16, n))


def unpack_weight(words, scales, fmt):
    g, _, n = scales.shape
    words = np.ascontiguousarray(words).reshape(g, 128, n, -1)
    if fmt == "e4m3":
        vals = words.view(ml_dtypes.float8_e4m3fn).astype(np.float64)
    else:
        nib = np.empty((g, 128, n, 4), np.uint8)
        nib[..., 0::2] = words & 0xF
        nib[..., 1::2] = words >> 4
        vals = E2M1[nib]
    vals = vals * np.repeat(np.exp2(scales.astype(np.float64) - 127.0), 8, axis=1)[..., None]
    return vals.transpose(0, 1, 3, 2).reshape(g * 512, n)


K, T, J, R, O, N = 512, 512, 256, 512, 128, 256


def setup_inputs():
    n = np.random.standard_normal
    idx = np.random.permutation(T)[:J]
    idx2 = np.random.permutation(J)[:O]
    idx3 = np.random.permutation(J)[:O]
    fk = mx_kscale(K)
    fr = mx_kscale(R)
    wp = pack_weight(n((K, R)) * 1 / np.sqrt(K) * fk[:, None] * fr, "e4m3")
    wbp = pack_weight(n((R, N)) * 1 / np.sqrt(R) / fr[:, None], "e2m1")
    return {
        "xf": (n((K, T))).astype(np.float32),
        "ow": (n((K, J)) * 0.7).astype(np.float32),
        "fk": (np.random.uniform(0.5, 2.0, (K, 1)) / fk[:, None]).astype(np.float32),
        "w_words": wp[0],
        "w_scales": wp[1],
        "wb_words": wbp[0],
        "wb_scales": wbp[1],
        "bi": (np.random.uniform(-0.5, 0.5, (1, N))).astype(np.float32),
        "offs": striped(idx),
        "offs2": striped(idx2),
        "offs3": striped(idx3),
    }


def reference(xf, ow, fk, w_words, w_scales, wb_words, wb_scales, bi, offs, offs2, offs3):
    idx = unstriped(offs)
    idx2 = unstriped(offs2)
    idx3 = unstriped(offs3)
    wu = unpack_weight(w_words, w_scales, "e4m3")
    wbu = unpack_weight(wb_words, wb_scales, "e2m1")
    u = (f64(xf)[:, idx] - f64(ow)) * f64(fk)
    uq = mxq(u, 0, "e4m3")
    a = wu.T @ uq
    hid = np.abs(a[:, idx2] - 0.5 * a[:, idx3])
    hidq = mxq(hid, 0, "e5m2")
    p = hidq.T @ wbu
    ea = np.exp(0.7 * p + f64(bi))
    y = 256.0 * ea / np.sum(ea, axis=1, keepdims=True)
    return y

@@ -1,0 +1,176 @@
+from contextlib import ExitStack
+
+import concourse.mybir as mybir
+from concourse.masks import make_identity
+
+K, T, J, R, O, N = 512, 512, 256, 512, 128, 256
+FLOPS = 2 * K * R * J + 2 * R * O * N
+
+F32 = mybir.dt.float32
+BF16 = mybir.dt.bfloat16
+I32 = mybir.dt.int32
+U32 = mybir.dt.uint32
+U16 = mybir.dt.uint16
+U8 = mybir.dt.uint8
+E4M3X4 = mybir.dt.float8_e4m3fn_x4
+E5M2X4 = mybir.dt.float8_e5m2_x4
+E2M1X4 = mybir.dt.float4_e2m1fn_x4
+ALU = mybir.AluOpType
+ACT = mybir.ActivationFunctionType
+AXIS = mybir.AxisListType
+
+P = 128
+PACK = 4
+QUADS = 4
+U_CUT = 168
+
+
+def load_scale_rows(queue, plane, rows):
+    for q in range(QUADS):
+        queue.dma_start(
+            out=plane[32 * q : 32 * q + 4, :].bitcast(I32),
+            in_=rows[4 * q : 4 * q + 4, :].bitcast(I32),
+        )
+
+
+def deal_columns(nc, dealt, raw, t0):
+    nc.vector.tensor_copy(
+        out=dealt[:].rearrange("p t m -> p m t")[:, :, t0 : t0 + 2],
+        in_=raw[:].rearrange("p (m t) -> p m t", t=PACK)[:, :, t0 : t0 + 2],
+    )
+
+
+def tile_list_looks_offsetpicks_farther_rowshares_kernel(
+    tc, xf, ow, fk, w_words, w_scales, wb_words, wb_scales, bi, offs, offs2, offs3, out
+):
+    nc = tc.nc
+    with ExitStack() as ctx:
+        sb = ctx.enter_context(tc.tile_pool(name="sb", bufs=1))
+        ps = ctx.enter_context(tc.psum_pool(name="ps", bufs=1))
+
+        list1 = sb.tile([P, J // 16], U16, name="list1")
+        list2 = sb.tile([P, O // 16], U16, name="list2")
+        list3 = sb.tile([P, O // 16], U16, name="list3")
+        fk_sb = sb.tile([P, PACK], F32, name="fk_sb")
+        bi_sb = sb.tile([P, 2], F32, name="bi_sb")
+        x_sb = [sb.tile([P, T], F32, name="x_sb%d" % t) for t in range(PACK)]
+        ow_sb = [sb.tile([P, 2, J], F32, name="ow_sb%d" % h) for h in range(2)]
+        w_raw = sb.tile([P, R], U32, name="w_raw")
+        ws_raw = sb.tile([P, R], U8, name="ws_raw")
+        w_codes = sb.tile([P, PACK, P], U32, name="w_codes", align_bytes=64)
+        w_plane = sb.tile([P, PACK, P], U8, name="w_plane", align_bytes=64)
+        wb_codes = sb.tile([P, 2 * N], U8, name="wb_codes", align_bytes=64)
+        wb_plane = sb.tile([P, N], U8, name="wb_plane", align_bytes=64)
+        ident = sb.tile([P, P], F32, name="ident")
+
+        nc.gpsimd.memset(ws_raw[:].bitcast(I32), 0)
+        nc.gpsimd.memset(wb_plane[:].bitcast(I32), 0)
+        nc.scalar.dma_start(out=fk_sb[:], in_=fk.rearrange("(p t) o -> p (t o)", t=PACK))
+        nc.scalar.dma_start(out=bi_sb[:], in_=bi.rearrange("o (p c) -> p (o c)", c=2))
+        make_identity(nc, ident[:])
+
+        x_rows = xf.rearrange("(p t) c -> p t c", t=PACK)
+        ow_rows = ow.rearrange("(p t) j -> p t j", t=PACK)
+        nc.sync.dma_start(list1[:], offs)
+        for t in range(PACK):
+            nc.sync.dma_start(out=x_sb[t][:], in_=x_rows[:, t, :])
+            if t % 2 == 0:
+                nc.sync.dma_start(out=ow_sb[t // 2][:], in_=ow_rows[:, t : t + 2, :])
+        nc.sync.dma_start(
+            out=w_raw[:].bitcast(I32), in_=w_words[0].rearrange("p c t -> p (c t)").bitcast(I32)
+        )
+        load_scale_rows(nc.sync, ws_raw, w_scales[0])
+        nc.sync.dma_start(list3[:], offs3)
+        nc.sync.dma_start(list2[:], offs2)
+        nc.sync.dma_start(out=wb_codes[:].bitcast(I32), in_=wb_words[0].bitcast(I32))
+        load_scale_rows(nc.sync, wb_plane, wb_scales[0])
+
+        bias_ps = ps.tile([P, 2, P], F32, name="bias_ps")
+        for c in range(2):
+            nc.tensor.transpose(bias_ps[:, c, :], bi_sb[:, c : c + 1].to_broadcast([P, P]), ident[:])
+        bias = sb.tile([P, P, 2], F32, name="bias")
+        nc.scalar.copy(out=bias[:], in_=bias_ps[:].rearrange("p c n -> p n c"))
+
+        u_bf = sb.tile([P, J, PACK], BF16, name="u_bf", align_bytes=64)
+        for t in range(PACK):
+            diff = sb.tile([P, J], F32, name="diff%d" % t)
+            nc.vector.tensor_tensor(
+                diff[:], x_sb[t][:].indirect(list1[:]), ow_sb[t // 2][:, t % 2, :], ALU.subtract
+            )
+            lo = 0 if t < 2 else U_CUT
+            nc.scalar.activation(out=u_bf[:, lo:, t], in_=diff[:, lo:], func=ACT.Copy, scale=fk_sb[:, t : t + 1])
+            if lo:
+                nc.vector.tensor_scalar(u_bf[:, :lo, t], diff[:, :lo], fk_sb[:, t : t + 1], None, ALU.mult)
+
+        deal_columns(nc, w_codes, w_raw, 0)
+        deal_columns(nc, w_plane, ws_raw, 0)
+        u_codes = sb.tile([P, J], U32, name="u_codes", align_bytes=64)
+        u_plane = sb.tile([P, J], U8, name="u_plane", align_bytes=64)
+        nc.vector.quantize_mx(
+            out=u_codes[:].bitcast(E4M3X4), scales=u_plane[:], in_=u_bf[:].rearrange("p j t -> p (j t)")
+        )
+
+        deal_columns(nc, w_codes, w_raw, 2)
+        deal_columns(nc, w_plane, ws_raw, 2)
+
+        signed = sb.tile([P, PACK, O], F32, name="signed")
+        a_ps = [ps.tile([P, J], F32, name="a_ps%d" % t) for t in range(PACK)]
+        a_sb = [sb.tile([P, J], F32, name="a_sb%d" % t) for t in range(PACK)]
+        for t in range(PACK):
+            nc.tensor.matmul_mx(
+                out=a_ps[t][:],
+                lhsT=w_codes[:, t, :].bitcast(E4M3X4),
+                lhsT_scale=w_plane[:, t, :],
+                rhs=u_codes[:].bitcast(E4M3X4),
+                rhs_scale=u_plane[:],
+                start=True,
+                stop=True,
+            )
+        for t in range(PACK):
+            if t < 2:
+                nc.scalar.copy(out=a_sb[t][:], in_=a_ps[t][:])
+            else:
+                nc.vector.tensor_copy(out=a_sb[t][:], in_=a_ps[t][:])
+        for t in range(PACK):
+            half = sb.tile([P, O], F32, name="half%d" % t)
+            nc.scalar.activation(out=half[:], in_=a_sb[t][:].indirect(list3[:]), func=ACT.Copy, scale=0.5)
+            nc.vector.tensor_tensor(signed[:, t, :], a_sb[t][:].indirect(list2[:]), half[:], ALU.subtract)
+
+        hid_bf = sb.tile([P, O, PACK], BF16, name="hid_bf", align_bytes=64)
+        woven = signed[:].rearrange("p t o -> p o t")
+        cut = O // 2
+        nc.scalar.activation(out=hid_bf[:, :, 0:2], in_=woven[:, :, 0:2], func=ACT.Abs)
+        nc.scalar.activation(out=hid_bf[:, :cut, 2:4], in_=woven[:, :cut, 2:4], func=ACT.Abs)
+        nc.vector.scalar_tensor_tensor(
+            hid_bf[:, cut:, 2:4], woven[:, cut:, 2:4], -1.0, woven[:, cut:, 2:4], ALU.mult, ALU.max
+        )
+        h_codes = sb.tile([P, O], U32, name="h_codes", align_bytes=64)
+        h_plane = sb.tile([P, O], U8, name="h_plane", align_bytes=64)
+        nc.vector.quantize_mx(
+            out=h_codes[:].bitcast(E5M2X4), scales=h_plane[:], in_=hid_bf[:].rearrange("p o t -> p (o t)")
+        )
+        p_ps = ps.tile([P, N], F32, name="p_ps")
+        nc.tensor.matmul_mx(
+            out=p_ps[:],
+            lhsT=h_codes[:].bitcast(E5M2X4),
+            lhsT_scale=h_plane[:],
+            rhs=wb_codes[:].bitcast(E2M1X4),
+            rhs_scale=wb_plane[:],
+            start=True,
+            stop=True,
+        )
+
+        logit = sb.tile([P, N], F32, name="logit")
+        nc.vector.scalar_tensor_tensor(
+            logit[:], p_ps[:], 0.7, bias[:].rearrange("p n c -> p (n c)"), ALU.mult, ALU.add
+        )
+        neg_max = sb.tile([P, 1], F32, name="neg_max")
+        nc.vector.tensor_reduce(out=neg_max[:], in_=logit[:], axis=AXIS.X, op=ALU.max, negate=True)
+        ea = sb.tile([P, N], F32, name="ea")
+        total = sb.tile([P, 1], F32, name="total")
+        nc.scalar.activation(out=ea[:], in_=logit[:], func=ACT.Exp, bias=neg_max[:], accum_out=total[:])
+        inv = sb.tile([P, 1], F32, name="inv")
+        nc.vector.reciprocal(out=inv[:], in_=total[:])
+        shares = sb.tile([P, N], F32, name="shares")
+        nc.vector.tensor_scalar(shares[:], ea[:], inv[:], 256.0, ALU.mult, ALU.mult)
+        nc.sync.dma_start(out=out, in_=shares[:])

@@ -54,12 +54,11 @@ def tile_list_looks_offsetpicks_farther_rowshares_kernel(
         fk_sb = sb.tile([P, PACK], F32, name="fk_sb")
         bi_sb = sb.tile([P, 2], F32, name="bi_sb")
         x_sb = [sb.tile([P, T], F32, name="x_sb%d" % t) for t in range(PACK)]
-        ow_sb = [sb.tile([P, 2, J], F32, name="ow_sb%d" % h) for h in range(2)]
+        ow_sb = [sb.tile([P, 2, J], F32, name="ow_sb%d" % h, tag="ow_sb%d" % h, align_bytes=64) for h in range(2)]
         w_raw = sb.tile([P, R], U32, name="w_raw")
         ws_raw = sb.tile([P, R], U8, name="ws_raw")
         w_codes = sb.tile([P, PACK, P], U32, name="w_codes", align_bytes=64)
         w_plane = sb.tile([P, PACK, P], U8, name="w_plane", align_bytes=64)
-        wb_codes = sb.tile([P, 2 * N], U8, name="wb_codes", align_bytes=64)
         wb_plane = sb.tile([P, N], U8, name="wb_plane", align_bytes=64)
         ident = sb.tile([P, P], F32, name="ident")
 
@@ -69,6 +68,8 @@ def tile_list_looks_offsetpicks_farther_rowshares_kernel(
         nc.scalar.dma_start(out=bi_sb[:], in_=bi.rearrange("o (p c) -> p (o c)", c=2))
         make_identity(nc, ident[:])
 
+        fk_act = sb.tile([P, PACK], F32, name="fk_act")
+        nc.scalar.activation(out=fk_act[:], in_=fk_sb[:], func=ACT.Copy)
         x_rows = xf.rearrange("(p t) c -> p t c", t=PACK)
         ow_rows = ow.rearrange("(p t) j -> p t j", t=PACK)
         nc.sync.dma_start(list1[:], offs)
@@ -82,7 +83,6 @@ def tile_list_looks_offsetpicks_farther_rowshares_kernel(
         load_scale_rows(nc.sync, ws_raw, w_scales[0])
         nc.sync.dma_start(list3[:], offs3)
         nc.sync.dma_start(list2[:], offs2)
-        nc.sync.dma_start(out=wb_codes[:].bitcast(I32), in_=wb_words[0].bitcast(I32))
         load_scale_rows(nc.sync, wb_plane, wb_scales[0])
 
         bias_ps = ps.tile([P, 2, P], F32, name="bias_ps")
@@ -98,10 +98,12 @@ def tile_list_looks_offsetpicks_farther_rowshares_kernel(
                 diff[:], x_sb[t][:].indirect(list1[:]), ow_sb[t // 2][:, t % 2, :], ALU.subtract
             )
             lo = 0 if t < 2 else U_CUT
-            nc.scalar.activation(out=u_bf[:, lo:, t], in_=diff[:, lo:], func=ACT.Copy, scale=fk_sb[:, t : t + 1])
+            nc.scalar.activation(out=u_bf[:, lo:, t], in_=diff[:, lo:], func=ACT.Copy, scale=fk_act[:, t : t + 1])
             if lo:
                 nc.vector.tensor_scalar(u_bf[:, :lo, t], diff[:, :lo], fk_sb[:, t : t + 1], None, ALU.mult)
 
+        wb_codes = sb.tile([P, 2 * N], U8, name="wb_codes", tag="ow_sb0", align_bytes=64)
+        nc.sync.dma_start(out=wb_codes[:].bitcast(I32), in_=wb_words[0].bitcast(I32))
         deal_columns(nc, w_codes, w_raw, 0)
         deal_columns(nc, w_plane, ws_raw, 0)
         u_codes = sb.tile([P, J], U32, name="u_codes", align_bytes=64)

from contextlib import ExitStack

import concourse.mybir as mybir
from concourse.masks import make_identity

K, T, J, R, O, N = 512, 512, 256, 512, 128, 256
FLOPS = 2 * K * R * J + 2 * R * O * N

F32 = mybir.dt.float32
BF16 = mybir.dt.bfloat16
I32 = mybir.dt.int32
U32 = mybir.dt.uint32
U16 = mybir.dt.uint16
U8 = mybir.dt.uint8
E4M3X4 = mybir.dt.float8_e4m3fn_x4
E5M2X4 = mybir.dt.float8_e5m2_x4
E2M1X4 = mybir.dt.float4_e2m1fn_x4
ALU = mybir.AluOpType
ACT = mybir.ActivationFunctionType
AXIS = mybir.AxisListType

P = 128
PACK = 4
QUADS = 4
U_CUT = 168


def load_scale_rows(queue, plane, rows):
    for q in range(QUADS):
        queue.dma_start(
            out=plane[32 * q : 32 * q + 4, :].bitcast(I32),
            in_=rows[4 * q : 4 * q + 4, :].bitcast(I32),
        )


def deal_columns(nc, dealt, raw, t0):
    nc.vector.tensor_copy(
        out=dealt[:].rearrange("p t m -> p m t")[:, :, t0 : t0 + 2],
        in_=raw[:].rearrange("p (m t) -> p m t", t=PACK)[:, :, t0 : t0 + 2],
    )


def tile_list_looks_offsetpicks_farther_rowshares_kernel(
    tc, xf, ow, fk, w_words, w_scales, wb_words, wb_scales, bi, offs, offs2, offs3, out
):
    nc = tc.nc
    with ExitStack() as ctx:
        sb = ctx.enter_context(tc.tile_pool(name="sb", bufs=1))
        ps = ctx.enter_context(tc.psum_pool(name="ps", bufs=1))

        list1 = sb.tile([P, J // 16], U16, name="list1")
        list2 = sb.tile([P, O // 16], U16, name="list2")
        list3 = sb.tile([P, O // 16], U16, name="list3")
        fk_sb = sb.tile([P, PACK], F32, name="fk_sb")
        bi_sb = sb.tile([P, 2], F32, name="bi_sb")
        x_sb = [sb.tile([P, T], F32, name="x_sb%d" % t) for t in range(PACK)]
        ow_sb = [sb.tile([P, 2, J], F32, name="ow_sb%d" % h, tag="ow_sb%d" % h, align_bytes=64) for h in range(2)]
        w_raw = sb.tile([P, R], U32, name="w_raw")
        ws_raw = sb.tile([P, R], U8, name="ws_raw")
        w_codes = sb.tile([P, PACK, P], U32, name="w_codes", align_bytes=64)
        w_plane = sb.tile([P, PACK, P], U8, name="w_plane", align_bytes=64)
        wb_plane = sb.tile([P, N], U8, name="wb_plane", align_bytes=64)
        ident = sb.tile([P, P], F32, name="ident")

        nc.gpsimd.memset(ws_raw[:].bitcast(I32), 0)
        nc.gpsimd.memset(wb_plane[:].bitcast(I32), 0)
        nc.scalar.dma_start(out=fk_sb[:], in_=fk.rearrange("(p t) o -> p (t o)", t=PACK))
        nc.scalar.dma_start(out=bi_sb[:], in_=bi.rearrange("o (p c) -> p (o c)", c=2))
        make_identity(nc, ident[:])

        fk_act = sb.tile([P, PACK], F32, name="fk_act")
        nc.scalar.activation(out=fk_act[:], in_=fk_sb[:], func=ACT.Copy)
        x_rows = xf.rearrange("(p t) c -> p t c", t=PACK)
        ow_rows = ow.rearrange("(p t) j -> p t j", t=PACK)
        nc.sync.dma_start(list1[:], offs)
        for t in range(PACK):
            nc.sync.dma_start(out=x_sb[t][:], in_=x_rows[:, t, :])
            if t % 2 == 0:
                nc.sync.dma_start(out=ow_sb[t // 2][:], in_=ow_rows[:, t : t + 2, :])
        nc.sync.dma_start(
            out=w_raw[:].bitcast(I32), in_=w_words[0].rearrange("p c t -> p (c t)").bitcast(I32)
        )
        load_scale_rows(nc.sync, ws_raw, w_scales[0])
        nc.sync.dma_start(list3[:], offs3)
        nc.sync.dma_start(list2[:], offs2)
        load_scale_rows(nc.sync, wb_plane, wb_scales[0])

        bias_ps = ps.tile([P, 2, P], F32, name="bias_ps")
        for c in range(2):
            nc.tensor.transpose(bias_ps[:, c, :], bi_sb[:, c : c + 1].to_broadcast([P, P]), ident[:])
        bias = sb.tile([P, P, 2], F32, name="bias")
        nc.scalar.copy(out=bias[:], in_=bias_ps[:].rearrange("p c n -> p n c"))

        u_bf = sb.tile([P, J, PACK], BF16, name="u_bf", align_bytes=64)
        for t in range(PACK):
            diff = sb.tile([P, J], F32, name="diff%d" % t)
            nc.vector.tensor_tensor(
                diff[:], x_sb[t][:].indirect(list1[:]), ow_sb[t // 2][:, t % 2, :], ALU.subtract
            )
            lo = 0 if t < 2 else U_CUT
            nc.scalar.activation(out=u_bf[:, lo:, t], in_=diff[:, lo:], func=ACT.Copy, scale=fk_act[:, t : t + 1])
            if lo:
                nc.vector.tensor_scalar(u_bf[:, :lo, t], diff[:, :lo], fk_sb[:, t : t + 1], None, ALU.mult)

        wb_codes = sb.tile([P, 2 * N], U8, name="wb_codes", tag="ow_sb0", align_bytes=64)
        nc.sync.dma_start(out=wb_codes[:].bitcast(I32), in_=wb_words[0].bitcast(I32))
        deal_columns(nc, w_codes, w_raw, 0)
        deal_columns(nc, w_plane, ws_raw, 0)
        u_codes = sb.tile([P, J], U32, name="u_codes", align_bytes=64)
        u_plane = sb.tile([P, J], U8, name="u_plane", align_bytes=64)
        nc.vector.quantize_mx(
            out=u_codes[:].bitcast(E4M3X4), scales=u_plane[:], in_=u_bf[:].rearrange("p j t -> p (j t)")
        )

        deal_columns(nc, w_codes, w_raw, 2)
        deal_columns(nc, w_plane, ws_raw, 2)

        signed = sb.tile([P, PACK, O], F32, name="signed")
        a_ps = [ps.tile([P, J], F32, name="a_ps%d" % t) for t in range(PACK)]
        a_sb = [sb.tile([P, J], F32, name="a_sb%d" % t) for t in range(PACK)]
        for t in range(PACK):
            nc.tensor.matmul_mx(
                out=a_ps[t][:],
                lhsT=w_codes[:, t, :].bitcast(E4M3X4),
                lhsT_scale=w_plane[:, t, :],
                rhs=u_codes[:].bitcast(E4M3X4),
                rhs_scale=u_plane[:],
                start=True,
                stop=True,
            )
        for t in range(PACK):
            if t < 2:
                nc.scalar.copy(out=a_sb[t][:], in_=a_ps[t][:])
            else:
                nc.vector.tensor_copy(out=a_sb[t][:], in_=a_ps[t][:])
        for t in range(PACK):
            half = sb.tile([P, O], F32, name="half%d" % t)
            nc.scalar.activation(out=half[:], in_=a_sb[t][:].indirect(list3[:]), func=ACT.Copy, scale=0.5)
            nc.vector.tensor_tensor(signed[:, t, :], a_sb[t][:].indirect(list2[:]), half[:], ALU.subtract)

        hid_bf = sb.tile([P, O, PACK], BF16, name="hid_bf", align_bytes=64)
        woven = signed[:].rearrange("p t o -> p o t")
        cut = O // 2
        nc.scalar.activation(out=hid_bf[:, :, 0:2], in_=woven[:, :, 0:2], func=ACT.Abs)
        nc.scalar.activation(out=hid_bf[:, :cut, 2:4], in_=woven[:, :cut, 2:4], func=ACT.Abs)
        nc.vector.scalar_tensor_tensor(
            hid_bf[:, cut:, 2:4], woven[:, cut:, 2:4], -1.0, woven[:, cut:, 2:4], ALU.mult, ALU.max
        )
        h_codes = sb.tile([P, O], U32, name="h_codes", align_bytes=64)
        h_plane = sb.tile([P, O], U8, name="h_plane", align_bytes=64)
        nc.vector.quantize_mx(
            out=h_codes[:].bitcast(E5M2X4), scales=h_plane[:], in_=hid_bf[:].rearrange("p o t -> p (o t)")
        )
        p_ps = ps.tile([P, N], F32, name="p_ps")
        nc.tensor.matmul_mx(
            out=p_ps[:],
            lhsT=h_codes[:].bitcast(E5M2X4),
            lhsT_scale=h_plane[:],
            rhs=wb_codes[:].bitcast(E2M1X4),
            rhs_scale=wb_plane[:],
            start=True,
            stop=True,
        )

        logit = sb.tile([P, N], F32, name="logit")
        nc.vector.scalar_tensor_tensor(
            logit[:], p_ps[:], 0.7, bias[:].rearrange("p n c -> p (n c)"), ALU.mult, ALU.add
        )
        neg_max = sb.tile([P, 1], F32, name="neg_max")
        nc.vector.tensor_reduce(out=neg_max[:], in_=logit[:], axis=AXIS.X, op=ALU.max, negate=True)
        ea = sb.tile([P, N], F32, name="ea")
        total = sb.tile([P, 1], F32, name="total")
        nc.scalar.activation(out=ea[:], in_=logit[:], func=ACT.Exp, bias=neg_max[:], accum_out=total[:])
        inv = sb.tile([P, 1], F32, name="inv")
        nc.vector.reciprocal(out=inv[:], in_=total[:])
        shares = sb.tile([P, N], F32, name="shares")
        nc.vector.tensor_scalar(shares[:], ea[:], inv[:], 256.0, ALU.mult, ALU.mult)
        nc.sync.dma_start(out=out, in_=shares[:])
